import numpy as np
import ml_dtypes


def mxq(x, axis, fmt="e4m3"):
    dtype, down = {"e4m3": (ml_dtypes.float8_e4m3fn, 7), "e5m2": (ml_dtypes.float8_e5m2, 14)}[fmt]
    v = np.moveaxis(np.asarray(x, np.float32).astype(ml_dtypes.bfloat16).astype(np.float64), axis, -1)
    blocks = v.reshape(v.shape[:-1] + (-1, 32))
    amax = np.abs(blocks).max(-1, keepdims=True)
    byte = np.maximum(np.where(amax > 0, np.frexp(amax)[1] - 1 + 127, 0) - down, 1)
    scale = np.exp2(byte - 127.0)
    codes = (blocks / scale).astype(np.float32).astype(dtype).astype(np.float64)
    return np.moveaxis((codes * scale).reshape(v.shape), -1, axis)


WIDE = False


def mx_kscale(k):
    if not WIDE:
        return np.ones(k)
    levels = np.array([10, -10, 5, -5, 0])
    if k % 512:
        return np.exp2(np.random.permutation(np.resize(levels, k // 32))).repeat(32)
    a = np.empty((k // 512, 16))
    for p in range(k // 512):
        a[p, :8] = np.random.permutation(np.resize(levels, 8))
        for g in range(8):
            far = levels[np.abs(levels - a[p, g]) >= 10]
            a[p, g + 8] = far[np.random.randint(len(far))]
    return np.exp2(a.ravel()).repeat(32)


def f64(x):
    return np.asarray(x).astype(np.float64)


def striped(idx):
    return np.tile(idx.reshape(-1, 16).T, (8, 1)).astype(np.uint16)


def unstriped(offs):
    return offs[:16].T.reshape(-1).astype(np.int64)


E2M1 = np.array([0.0, 0.5, 1.0, 1.5, 2.0, 3.0, 4.0, 6.0, -0.0, -0.5, -1.0, -1.5, -2.0, -3.0, -4.0, -6.0])


def pack_weight(w, fmt):
    k, n = w.shape
    w = f64(np.asarray(w, np.float32).astype(ml_dtypes.bfloat16)).reshape(k // 32, 32, n)
    amax = np.abs(w).max(1)
    if fmt == "e4m3":
        byte = np.frexp(amax)[1] - 1 + 127 - 7
    else:
        mant, ex = np.frexp(amax / 6.0)
        byte = np.where(mant > 0.5, ex, ex - 1) + 127
    byte = np.clip(np.where(amax > 0, byte, 1), 1, 254)
    scaled = (w * np.exp2(127.0 - byte)[:, None, :]).reshape(k, n).astype(np.float32)
    by_word = np.ascontiguousarray(scaled.reshape(k // 512, 128, 4, n).transpose(0, 1, 3, 2))
    if fmt == "e4m3":
        words = by_word.astype(ml_dtypes.float8_e4m3fn).view(np.uint8)
    else:
        c = by_word.astype(ml_dtypes.float4_e2m1fn).view(np.uint8) & 0xF
        words = (c[..., 0::2] | (c[..., 1::2] << 4)).reshape(k // 512, 128, 2 * n)
    return np.ascontiguousarray(words), np.ascontiguousarray(byte.astype(np.uint8).reshape(k // 512, 16, n))


def unpack_weight(words, scales, fmt):
    g, _, n = scales.shape
    words = np.ascontiguousarray(words).reshape(g, 128, n, -1)
    if fmt == "e4m3":
        vals = words.view(ml_dtypes.float8_e4m3fn).astype(np.float64)
    else:
        nib = np.empty((g, 128, n, 4), np.uint8)
        nib[..., 0::2] = words & 0xF
        nib[..., 1::2] = words >> 4
        vals = E2M1[nib]
    vals = vals * np.repeat(np.exp2(scales.astype(np.float64) - 127.0), 8, axis=1)[..., None]
    return vals.transpose(0, 1, 3, 2).reshape(g * 512, n)


def silu(v):
    return v / (1.0 + np.exp(-np.maximum(v, -700.0)))


def d_silu(v):
    s = 1.0 / (1.0 + np.exp(-np.maximum(v, -700.0)))
    return s * (1.0 + v * (1.0 - s))


K, T, E, C, H, N = 384, 640, 5, 256, 1024, 512


def by_expert(wq, xq):
    return np.concatenate([wq[e].T @ xq[:, e * C:(e + 1) * C] for e in range(E)], axis=1)


def setup_inputs():
    n = np.random.standard_normal
    s = mx_kscale(N)[:, None]
    u = mx_kscale(H)
    first = np.random.permutation(np.repeat(np.arange(E), T // E))
    second = (first + 1 + np.random.permutation(np.repeat(np.arange(E - 1), -(-T // (E - 1)))[:T])) % E
    while np.bincount(second, minlength=E).max() != T // E:
        load = np.bincount(second, minlength=E); hi, lo = int(load.argmax()), int(load.argmin())
        t = np.flatnonzero((second == hi) & (first != lo))[0]; second[t] = lo
    slot_token = np.empty(E * C, np.int64); pos = np.empty((2, T), np.int64); fill = np.zeros(E, np.int64)
    place = np.stack([np.random.permutation(C) for _ in range(E)])
    for r, deal in enumerate((first, second)):
        for t in np.random.permutation(T):
            e = deal[t]; j = e * C + place[e, fill[e]]; fill[e] += 1; slot_token[j] = t; pos[r, t] = j
    g = np.random.uniform(0.2, 0.8, T)
    w_slot = np.empty(E * C); w_slot[pos[0]] = g; w_slot[pos[1]] = 1.0 - g
    dy = pack_weight(n((N, T)) * s, "e4m3")
    return {
        "dy_words": dy[0],
        "dy_scales": dy[1],
        "a1": n((H, E * C)).astype(np.float32),
        "a3": n((H, E * C)).astype(np.float32),
        "w2": (n((E, N, H)) / np.sqrt(N) / s[None] * u[None, None, :]).astype(np.float32),
        "w1": (n((E, H, K)) / np.sqrt(H) / u[None, :, None]).astype(np.float32),
        "w3": (n((E, H, K)) / np.sqrt(H) / u[None, :, None]).astype(np.float32),
        "gate": np.tile(w_slot, (H, 1)).astype(np.float32),
        "offs": striped(slot_token),
        "pos1": striped(pos[0]),
        "pos2": striped(pos[1]),
    }


def reference(dy_words, dy_scales, a1, a3, w2, w1, w3, gate, offs, pos1, pos2):
    idx = unstriped(offs)
    gq = unpack_weight(dy_words, dy_scales, "e4m3")[:, idx]
    dh = f64(gate) * by_expert(mxq(f64(w2), 1, "e4m3"), gq)
    da1 = dh * f64(a3) * d_silu(f64(a1))
    da3 = dh * silu(f64(a1))
    dx = by_expert(mxq(f64(w1), 1, "e4m3"), mxq(da1, 0, "e4m3")) + by_expert(mxq(f64(w3), 1, "e4m3"), mxq(da3, 0, "e4m3"))
    return dx[:, unstriped(pos1)] + dx[:, unstriped(pos2)]

@@ -1,0 +1,305 @@
+from contextlib import ExitStack
+
+import concourse.mybir as mybir
+from concourse.masks import make_identity
+
+PR = {'sums': 2, 'turned': 2, 'acc': 3, 'gated': 6, 'q': 4, 'z': 2, 'th': 2, 'v': 5, 'up': 1, 'w2_b': 2, 'w2_c': 2, 'da_b': 1, 'w13_b': 3, 'wraw': 8, 'vc': (128, 128, 512, 0, 512, 384, 512, 384, 512, 128), 'early': (384, 384, 384, 256, 128), 'late': ((3, 2), (4, 1), (4, 2)), 'B': 1, 'A': 2, 'D': 1, 'lv': ((3, 1, 1), (4, 1, 1)), 'loads': ['w2', 'h1', 'h0', 'a1', 'a3'], 'steps': ['q', 'q13', 'da', 'act', 'qw2', 'mm1', 'qda', 'back']}
+K, T, E, C, H, N = 384, 640, 5, 256, 1024, 512
+S = E * C
+
+FLOPS = 2 * S * (N * H + 2 * H * K)
+BYTES = 4 * (2 * H * S + E * N * H + 2 * E * H * K + S + K * T) + N * T + 16 * T + 2 * 128 * (S + 2 * T) // 16
+
+F32 = mybir.dt.float32
+BF16 = mybir.dt.bfloat16
+I32 = mybir.dt.int32
+U32 = mybir.dt.uint32
+U16 = mybir.dt.uint16
+U8 = mybir.dt.uint8
+FP8X4 = mybir.dt.float8_e4m3fn_x4
+ALU = mybir.AluOpType
+ACT = mybir.ActivationFunctionType
+
+P = 128
+PACK = 4
+PASS = P * PACK
+HALVES = H // PASS
+K_TILES = K // P
+QUANT = 2048
+
+
+def by_fours_out(ap):
+    return ap.rearrange("p (c i t) -> p c t i", i=2, t=PACK)
+
+
+def by_fours_in(ap):
+    return ap.rearrange("p t (c i) -> p c t i", i=2)
+
+
+def tile_moe_bdx_glu_silu_kernel(
+    tc, dy_words, dy_scales, a1, a3, w2, w1, w3, gate, offs, pos1, pos2, out
+):
+    nc = tc.nc
+    with ExitStack() as ctx:
+        held = ctx.enter_context(tc.tile_pool(name="held", bufs=1))
+        ring2 = ctx.enter_context(tc.tile_pool(name="ring2", bufs=2))
+        ring3 = ctx.enter_context(tc.tile_pool(name="ring3", bufs=3))
+        ring4 = ctx.enter_context(tc.tile_pool(name="ring4", bufs=4))
+        ring5 = ctx.enter_context(tc.tile_pool(name="ring5", bufs=5))
+        wraw = ctx.enter_context(tc.tile_pool(name="wraw", bufs=8))
+        psum4 = ctx.enter_context(tc.psum_pool(name="psum4", bufs=4))
+        psum2 = ctx.enter_context(tc.psum_pool(name="psum2", bufs=2))
+
+        offs_sb = held.tile([P, S // 16], U16, name="offs_sb")
+        pos1_sb = held.tile([P, T // 16], U16, name="pos1_sb")
+        pos2_sb = held.tile([P, T // 16], U16, name="pos2_sb")
+        dy_w = held.tile([P, T], I32, name="dy_w", align_bytes=64)
+        dy_s = held.tile([P, T], U8, name="dy_s", align_bytes=64)
+        gate_rows = held.tile([P, P], F32, name="gate_rows")
+        ident = held.tile([P, P], F32, name="ident")
+        half_gate = held.tile([P, S // P], F32, name="half_gate")
+        g_w = [held.tile([P, C], U32, name="g_w%d" % e, align_bytes=64) for e in range(E)]
+        g_s = [held.tile([P, C], U8, name="g_s%d" % e, align_bytes=64) for e in range(E)]
+        dx = [held.tile([P, S], F32, name="dx%d" % kt, align_bytes=64) for kt in range(K_TILES)]
+
+        make_identity(nc, ident[:])
+
+        nc.sync.dma_start(offs_sb[:], offs)
+        nc.sync.dma_start(dy_w[:], dy_words[0].rearrange("p t d -> p (t d)").bitcast(I32))
+        for quad in range(4):
+            rows = dy_scales[0, 4 * quad : 4 * quad + 4, :].bitcast(I32)
+            nc.sync.dma_start(
+                dy_s[32 * quad : 32 * quad + 32, :].bitcast(I32), rows.unsqueeze(0).broadcast_to([8, 4, T // 4])
+            )
+
+        def load_gate():
+            nc.sync.dma_start(gate_rows[:], gate.rearrange("i (c p) -> (i c) p", p=P)[0:P, :])
+            gate_ps = psum4.tile([P, PACK, P], F32, name="turned", bufs=PR["turned"])
+            nc.tensor.transpose(gate_ps[:, 0, :], gate_rows[:], ident[:])
+            nc.scalar.activation(half_gate[:], gate_ps[:, 0, 0 : S // P], ACT.Copy, scale=0.5)
+
+        da_codes = {}
+        da_scales = {}
+        raw13 = {}
+
+        def gather_gradients(e):
+            entries = offs_sb[:, e * (C // 16) : (e + 1) * (C // 16)]
+            nc.vector.tensor_copy(g_w[e][:], dy_w[:].bitcast(U32).indirect(entries))
+            nc.vector.tensor_copy(g_s[e][:], dy_s[:].indirect(entries))
+
+        def cast(on_vector, dst, src, negate):
+            if on_vector and negate:
+                nc.vector.tensor_scalar(by_fours_out(dst), by_fours_in(src), -1.0, None, ALU.mult)
+            elif on_vector:
+                nc.vector.tensor_copy(by_fours_out(dst), by_fours_in(src))
+            else:
+                nc.scalar.activation(by_fours_out(dst), by_fours_in(src), ACT.Copy, scale=-1.0 if negate else 1.0)
+
+        w2_raw, v, up, th, z, q, w2_c, w2_s = {}, {}, {}, {}, {}, {}, {}, {}
+
+        def load_w2(u):
+            e, h = divmod(u, HALVES)
+            w2_raw[u] = wraw.tile([P, PACK, PASS], F32, name="w_raw", bufs=PR["wraw"])
+            nc.sync.dma_start(w2_raw[u][:], w2[e][:, h * PASS : (h + 1) * PASS].rearrange("(p j) c -> p j c", j=PACK))
+
+        def load_saved(u, which):
+            e, h = divmod(u, HALVES)
+            src = (a1, a3)[which][h * PASS : (h + 1) * PASS, e * C : (e + 1) * C]
+            if which == 0:
+                dst = v[u] = ring4.tile([P, PACK, C], F32, name="v", bufs=PR["v"])
+            else:
+                dst = up[u] = ring3.tile([P, PACK, C], F32, name="up", bufs=PR["up"])
+            nc.sync.dma_start(dst[:], src.rearrange("(p t) c -> p t c", t=PACK))
+
+        def quantise_w2(u, split):
+            w2_b = ring2.tile([P, PASS * PACK], BF16, name="w2_b", align_bytes=64, bufs=PR["w2_b"])
+            if split < PASS:
+                cast(False, w2_b[:, split * PACK :], w2_raw[u][:, :, split:], False)
+            if split > 0:
+                cast(True, w2_b[:, : split * PACK], w2_raw[u][:, :, :split], False)
+            w2_c[u] = ring2.tile([P, PASS], U32, name="w2_c", align_bytes=64, bufs=PR["w2_c"])
+            w2_s[u] = ring2.tile([P, PASS], U8, name="w2_s", align_bytes=64, bufs=PR["w2_c"])
+            nc.vector.quantize_mx(out=w2_c[u][:].bitcast(FP8X4), scales=w2_s[u][:], in_=w2_b[:])
+
+        def activations(u):
+            z[u] = ring3.tile([P, PACK, C], F32, name="z", bufs=PR["z"])
+            nc.scalar.activation(z[u][:], v[u][:], ACT.Silu, scale=-1.0)
+            th[u] = ring3.tile([P, PACK, C], F32, name="th", bufs=PR["th"])
+            nc.scalar.activation(th[u][:], v[u][:], ACT.Tanh, scale=0.5)
+            nc.vector.scalar_tensor_tensor(z[u][:], z[u][:], 1.0, up[u][:], ALU.subtract, ALU.mult)
+
+        turned = {}
+
+        def first_product(u):
+            e = u // HALVES
+            for s in range(C // P):
+                cols = slice(s * P, (s + 1) * P)
+                sums = psum2.tile([P, PASS], F32, name="sums", bufs=PR["sums"])
+                nc.tensor.matmul_mx(
+                    out=sums[:],
+                    lhsT=g_w[e][:, cols].bitcast(FP8X4),
+                    lhsT_scale=g_s[e][:, cols],
+                    rhs=w2_c[u][:].bitcast(FP8X4),
+                    rhs_scale=w2_s[u][:],
+                    start=True,
+                    stop=True,
+                )
+                gated = ring4.tile([P, PACK, P], F32, name="gated", bufs=PR["gated"])
+                block = e * (C // P) + s
+                nc.scalar.activation(
+                    gated[:],
+                    sums[:].rearrange("p (m t) -> p t m", t=PACK),
+                    ACT.Copy,
+                    scale=half_gate[:, block : block + 1],
+                )
+                turned[(u, s)] = psum4.tile([P, PACK, P], F32, name="turned", bufs=PR["turned"])
+                for t in range(PACK):
+                    nc.tensor.transpose(turned[(u, s)][:, t, :], gated[:, t, :], ident[:])
+
+        def times_sigmoid(u):
+            q[u] = ring2.tile([P, PACK, C], F32, name="q", bufs=PR["q"])
+            for s in range(C // P):
+                cols = slice(s * P, (s + 1) * P)
+                nc.vector.scalar_tensor_tensor(
+                    q[u][:, :, cols], th[u][:, :, cols], 1.0, turned[(u, s)][:], ALU.add, ALU.mult
+                )
+
+        da_b = {}
+
+        def products(u):
+            da_b[u] = ring2.tile([P, 2, C * PACK], BF16, name="da_b", align_bytes=64, bufs=PR["da_b"])
+            for m, factor in enumerate((z[u], v[u])):
+                nc.vector.tensor_tensor(
+                    by_fours_out(da_b[u][:, m, :]), by_fours_in(q[u][:]), by_fours_in(factor[:]), ALU.mult
+                )
+
+        def quantise_da(u):
+            codes = ring5.tile([P, 2 * C], U32, name="da_c", align_bytes=64)
+            scales = ring5.tile([P, 2 * C], U8, name="da_s", align_bytes=64)
+            nc.vector.quantize_mx(
+                out=codes[:].bitcast(FP8X4), scales=scales[:], in_=da_b[u][:].rearrange("p a c -> p (a c)")
+            )
+            da_codes[divmod(u, HALVES)] = codes
+            da_scales[divmod(u, HALVES)] = scales
+
+        def load13(e, m, k0, k1, halves=(0, 1)):
+            if k1 - k0 > 0:
+                for h in halves:
+                    raw = wraw.tile([P, PACK, k1 - k0], F32, name="w_raw", bufs=PR["wraw"])
+                    rows = (w1, w3)[m][e][h * PASS : (h + 1) * PASS, k0:k1]
+                    nc.sync.dma_start(raw[:], rows.rearrange("(p j) k -> p j k", j=PACK))
+                    raw13[(e, m, h, k0)] = raw[:]
+            else:
+                raw = wraw.tile([P, HALVES, PACK, k1 - k0], F32, name="w_raw", bufs=PR["wraw"])
+                for h in range(HALVES):
+                    rows = (w1, w3)[m][e][h * PASS : (h + 1) * PASS, k0:k1]
+                    nc.sync.dma_start(raw[:, h], rows.rearrange("(p j) k -> p j k", j=PACK))
+                    raw13[(e, m, h, k0)] = raw[:, h]
+
+        w13_c = {}
+        w13_s = {}
+
+        def quantise13(e, m, k0, k1, on_vector=False):
+            width = k1 - k0
+            words = HALVES * width
+            w_b = ring3.tile([P, words * PACK], BF16, name="w13_b", align_bytes=64, bufs=PR["w13_b"])
+            for h in range(HALVES):
+                cast(on_vector, w_b[:, h * width * PACK : (h + 1) * width * PACK], raw13[(e, m, h, k0)], m == 0)
+            w_c = ring4.tile([P, words], U32, name="w13_c", align_bytes=64)
+            w_s = ring4.tile([P, words], U8, name="w13_s", align_bytes=64)
+            for c0 in range(0, words, QUANT // PACK):
+                c1 = min(words, c0 + QUANT // PACK)
+                nc.vector.quantize_mx(
+                    out=w_c[:, c0:c1].bitcast(FP8X4), scales=w_s[:, c0:c1], in_=w_b[:, PACK * c0 : PACK * c1]
+                )
+            w13_c[(e, m, k0)] = w_c
+            w13_s[(e, m, k0)] = w_s
+
+        def back(e, k0, k1):
+            width = k1 - k0
+            for kt in range(k0 // P, k1 // P):
+                acc = psum2.tile([P, C], F32, name="acc", bufs=PR["acc"])
+                steps = [(h, m) for m in range(2) for h in range(HALVES)]
+                for n, (h, m) in enumerate(steps):
+                    c0 = h * width + kt * P - k0
+                    nc.tensor.matmul_mx(
+                        out=acc[:],
+                        lhsT=w13_c[(e, m, k0)][:, c0 : c0 + P].bitcast(FP8X4),
+                        lhsT_scale=w13_s[(e, m, k0)][:, c0 : c0 + P],
+                        rhs=da_codes[(e, h)][:, m * C : (m + 1) * C].bitcast(FP8X4),
+                        rhs_scale=da_scales[(e, h)][:, m * C : (m + 1) * C],
+                        start=n == 0,
+                        stop=n == len(steps) - 1,
+                    )
+                nc.scalar.copy(dx[kt][:, e * C : (e + 1) * C], acc[:])
+
+        def combine(kt):
+            first = ring2.tile([P, T], F32, name="first")
+            second = ring2.tile([P, T], F32, name="second")
+            nc.vector.tensor_copy(first[:], dx[kt][:].indirect(pos1_sb[:]))
+            nc.vector.tensor_copy(second[:], dx[kt][:].indirect(pos2_sb[:]))
+            nc.vector.tensor_tensor(first[:], first[:], second[:], ALU.add)
+            nc.sync.dma_start(out[kt * P : (kt + 1) * P, :], first[:])
+
+        units = E * HALVES
+        last = E - 1
+        VCAST, early, late, B, A = PR["vc"], PR["early"], PR["late"], PR["B"], PR["A"]
+        load_saved(0, 0)
+        load_w2(0)
+        load_gate()
+        load_saved(0, 1)
+        gather_gradients(0)
+        activations(0)
+        quantise_w2(0, VCAST[0])
+        first_product(0)
+        for u in range(1, A):
+            load_w2(u)
+            gather_gradients(u // 2) if u % 2 == 0 else None
+            quantise_w2(u, VCAST[u])
+            first_product(u)
+        for b in range(0, -B):
+            load13(*divmod(b, HALVES), 0, early[b // HALVES])
+            quantise13(*divmod(b, HALVES), 0, early[b // HALVES])
+        for u in range(units + max(B, 0)):
+            b = u - B
+            d = u - max(B, 0) - PR["D"]
+            for step in PR["loads"]:
+                if step == "w2" and u + A < units:
+                    load_w2(u + A)
+                if step == "a1" and u + 1 < units:
+                    load_saved(u + 1, 0)
+                if step == "a3" and u + 1 < units:
+                    load_saved(u + 1, 1)
+                if step in ("h0", "h1") and 0 <= b < units:
+                    load13(*divmod(b, HALVES), 0, early[b // HALVES], (int(step[1]),))
+            if u == 2:
+                nc.sync.dma_start(pos1_sb[:], pos1)
+                nc.sync.dma_start(pos2_sb[:], pos2)
+            if (u + A) % 2 == 0 and u + A < units:
+                gather_gradients((u + A) // 2)
+            for step in PR["steps"]:
+                if step == "q" and u < units:
+                    times_sigmoid(u)
+                if step == "qw2" and u + A < units:
+                    quantise_w2(u + A, VCAST[u + A])
+                if step == "da" and u < units:
+                    products(u)
+                if step == "act" and u + 1 < units:
+                    activations(u + 1)
+                if step == "mm1" and u + A < units:
+                    first_product(u + A)
+                if step == "q13" and 0 <= b < units:
+                    quantise13(*divmod(b, HALVES), 0, early[b // HALVES])
+                if step == "qda" and u < units:
+                    quantise_da(u)
+                if step == "back" and d >= 0 and d % HALVES == 1:
+                    back(d // HALVES, 0, early[d // HALVES])
+        if PR["D"] == 1:
+            back(last, 0, early[last])
+        for e, kt in late:
+            for m in range(2):
+                load13(e, m, kt * P, (kt + 1) * P)
+                quantise13(e, m, kt * P, (kt + 1) * P, (e, kt, m) in PR["lv"])
+            back(e, kt * P, (kt + 1) * P)
+        for kt in range(K_TILES):
+            combine(kt)

@@ -3,7 +3,7 @@ from contextlib import ExitStack
 import concourse.mybir as mybir
 from concourse.masks import make_identity
 
-PR = {'sums': 2, 'turned': 2, 'acc': 3, 'gated': 6, 'q': 4, 'z': 2, 'th': 2, 'v': 5, 'up': 1, 'w2_b': 2, 'w2_c': 2, 'da_b': 1, 'w13_b': 3, 'wraw': 8, 'vc': (128, 128, 512, 0, 512, 384, 512, 384, 512, 128), 'early': (384, 384, 384, 256, 128), 'late': ((3, 2), (4, 1), (4, 2)), 'B': 1, 'A': 2, 'D': 1, 'lv': ((3, 1, 1), (4, 1, 1)), 'loads': ['w2', 'h1', 'h0', 'a1', 'a3'], 'steps': ['q', 'q13', 'da', 'act', 'qw2', 'mm1', 'qda', 'back']}
+PR = {'sums': 2, 'turned': 2, 'acc': 4, 'gated': 4, 'q': 3, 'z': 2, 'th': 3, 'v': 3, 'up': 1, 'w2_b': 2, 'w2_c': 3, 'da_b': 1, 'w13_b': 3, 'wraw': 8, 'w2raw': 2, 'da_c': 6, 'w13_c': 5, 'vc': (0, 384, 0, 512, 512, 0, 512, 512, 512, 512), 'early': (384, 384, 384, 384, 128), 'loaded': (384, 384, 384, 384, 128), 'late': ((4, 1), (4, 2)), 'B': 1, 'A': 4, 'M': 1, 'D': 3, 'LW': 3, 'LA': 0, 'lv': ((5, 1), (6, 0), (6, 1), (8, 2), (9, 1)), 'w2split': 0, 'chunks': ((0,), (1, 2), (3, 4)), 'loads': ['a1', 'w2', 'a3', 'h0', 'h1'], 'steps': ['q', 'da', 'qda', 'q13', 'mm1', 'qw2', 'act', 'back', 'z'], 'gadd': 0, 'cut': 448, 'head': ['dy', 'w2', 'a1', 'gate', 'a3'], 'fix': 1}
 K, T, E, C, H, N = 384, 640, 5, 256, 1024, 512
 S = E * C
 
@@ -47,6 +47,7 @@ def tile_moe_bdx_glu_silu_kernel(
         ring4 = ctx.enter_context(tc.tile_pool(name="ring4", bufs=4))
         ring5 = ctx.enter_context(tc.tile_pool(name="ring5", bufs=5))
         wraw = ctx.enter_context(tc.tile_pool(name="wraw", bufs=8))
+        w2pool = ctx.enter_context(tc.tile_pool(name="w2pool", bufs=2))
         psum4 = ctx.enter_context(tc.psum_pool(name="psum4", bufs=4))
         psum2 = ctx.enter_context(tc.psum_pool(name="psum2", bufs=2))
 
@@ -64,13 +65,15 @@ def tile_moe_bdx_glu_silu_kernel(
 
         make_identity(nc, ident[:])
 
-        nc.sync.dma_start(offs_sb[:], offs)
-        nc.sync.dma_start(dy_w[:], dy_words[0].rearrange("p t d -> p (t d)").bitcast(I32))
-        for quad in range(4):
-            rows = dy_scales[0, 4 * quad : 4 * quad + 4, :].bitcast(I32)
-            nc.sync.dma_start(
-                dy_s[32 * quad : 32 * quad + 32, :].bitcast(I32), rows.unsqueeze(0).broadcast_to([8, 4, T // 4])
-            )
+
+        def load_dy():
+            nc.sync.dma_start(offs_sb[:], offs)
+            nc.sync.dma_start(dy_w[:], dy_words[0].rearrange("p t d -> p (t d)").bitcast(I32))
+            for quad in range(4):
+                rows = dy_scales[0, 4 * quad : 4 * quad + 4, :].bitcast(I32)
+                nc.sync.dma_start(
+                    dy_s[32 * quad : 32 * quad + 32, :].bitcast(I32), rows.unsqueeze(0).broadcast_to([8, 4, T // 4])
+                )
 
         def load_gate():
             nc.sync.dma_start(gate_rows[:], gate.rearrange("i (c p) -> (i c) p", p=P)[0:P, :])
@@ -95,21 +98,32 @@ def tile_moe_bdx_glu_silu_kernel(
             else:
                 nc.scalar.activation(by_fours_out(dst), by_fours_in(src), ACT.Copy, scale=-1.0 if negate else 1.0)
 
+        order = [(e, h) for group in PR["chunks"] for h in range(HALVES) for e in group]
         w2_raw, v, up, th, z, q, w2_c, w2_s = {}, {}, {}, {}, {}, {}, {}, {}
 
-        def load_w2(u):
-            e, h = divmod(u, HALVES)
-            w2_raw[u] = wraw.tile([P, PACK, PASS], F32, name="w_raw", bufs=PR["wraw"])
-            nc.sync.dma_start(w2_raw[u][:], w2[e][:, h * PASS : (h + 1) * PASS].rearrange("(p j) c -> p j c", j=PACK))
+        def load_w2(e, halves):
+            if len(halves) == HALVES:
+                raw = w2pool.tile([P, PACK, H], F32, name="w2_raw", bufs=PR["w2raw"])
+                nc.sync.dma_start(raw[:], w2[e].rearrange("(p j) c -> p j c", j=PACK))
+                for h in halves:
+                    w2_raw[HALVES * e + h] = raw[:, :, h * PASS : (h + 1) * PASS]
+            else:
+                h = halves[0]
+                raw = w2pool.tile([P, PACK, PASS], F32, name="w2_raw", bufs=PR["w2raw"])
+                nc.sync.dma_start(raw[:], w2[e][:, h * PASS : (h + 1) * PASS].rearrange("(p j) c -> p j c", j=PACK))
+                w2_raw[HALVES * e + h] = raw[:]
 
         def load_saved(u, which):
-            e, h = divmod(u, HALVES)
-            src = (a1, a3)[which][h * PASS : (h + 1) * PASS, e * C : (e + 1) * C]
+            e, h = order[u]
+            group = [g for g in PR["chunks"] if e in g][0]
+            src = (a1, a3)[which][h * PASS : (h + 1) * PASS, group[0] * C : (group[-1] + 1) * C]
             if which == 0:
-                dst = v[u] = ring4.tile([P, PACK, C], F32, name="v", bufs=PR["v"])
+                dst = ring4.tile([P, PACK, len(group) * C], F32, name="v", bufs=PR["v"])
             else:
-                dst = up[u] = ring3.tile([P, PACK, C], F32, name="up", bufs=PR["up"])
+                dst = ring3.tile([P, PACK, len(group) * C], F32, name="up", bufs=PR["up"])
             nc.sync.dma_start(dst[:], src.rearrange("(p t) c -> p t c", t=PACK))
+            for n, member in enumerate(group):
+                (v, up)[which][order.index((member, h))] = dst[:, :, n * C : (n + 1) * C]
 
         def quantise_w2(u, split):
             w2_b = ring2.tile([P, PASS * PACK], BF16, name="w2_b", align_bytes=64, bufs=PR["w2_b"])
@@ -123,15 +137,18 @@ def tile_moe_bdx_glu_silu_kernel(
 
         def activations(u):
             z[u] = ring3.tile([P, PACK, C], F32, name="z", bufs=PR["z"])
-            nc.scalar.activation(z[u][:], v[u][:], ACT.Silu, scale=-1.0)
+            nc.scalar.activation(z[u][:], v[u], ACT.Silu, scale=-1.0)
             th[u] = ring3.tile([P, PACK, C], F32, name="th", bufs=PR["th"])
-            nc.scalar.activation(th[u][:], v[u][:], ACT.Tanh, scale=0.5)
-            nc.vector.scalar_tensor_tensor(z[u][:], z[u][:], 1.0, up[u][:], ALU.subtract, ALU.mult)
+            nc.scalar.activation(th[u][:], v[u], ACT.Tanh, scale=0.5)
+
+        def times_up(u):
+            nc.vector.scalar_tensor_tensor(z[u][:], z[u][:], 1.0, up[u], ALU.subtract, ALU.mult)
 
         turned = {}
 
         def first_product(u):
-            e = u // HALVES
+            e, h = order[u]
+            j = HALVES * e + h
             for s in range(C // P):
                 cols = slice(s * P, (s + 1) * P)
                 sums = psum2.tile([P, PASS], F32, name="sums", bufs=PR["sums"])
@@ -139,8 +156,8 @@ def tile_moe_bdx_glu_silu_kernel(
                     out=sums[:],
                     lhsT=g_w[e][:, cols].bitcast(FP8X4),
                     lhsT_scale=g_s[e][:, cols],
-                    rhs=w2_c[u][:].bitcast(FP8X4),
-                    rhs_scale=w2_s[u][:],
+                    rhs=w2_c[j][:].bitcast(FP8X4),
+                    rhs_scale=w2_s[j][:],
                     start=True,
                     stop=True,
                 )
@@ -157,7 +174,7 @@ def tile_moe_bdx_glu_silu_kernel(
                     nc.tensor.transpose(turned[(u, s)][:, t, :], gated[:, t, :], ident[:])
 
         def times_sigmoid(u):
-            q[u] = ring2.tile([P, PACK, C], F32, name="q", bufs=PR["q"])
+            q[u] = th[u]
             for s in range(C // P):
                 cols = slice(s * P, (s + 1) * P)
                 nc.vector.scalar_tensor_tensor(
@@ -168,33 +185,27 @@ def tile_moe_bdx_glu_silu_kernel(
 
         def products(u):
             da_b[u] = ring2.tile([P, 2, C * PACK], BF16, name="da_b", align_bytes=64, bufs=PR["da_b"])
-            for m, factor in enumerate((z[u], v[u])):
+            for m, factor in enumerate((z[u][:], v[u])):
                 nc.vector.tensor_tensor(
-                    by_fours_out(da_b[u][:, m, :]), by_fours_in(q[u][:]), by_fours_in(factor[:]), ALU.mult
+                    by_fours_out(da_b[u][:, m, :]), by_fours_in(q[u][:]), by_fours_in(factor), ALU.mult
                 )
 
         def quantise_da(u):
-            codes = ring5.tile([P, 2 * C], U32, name="da_c", align_bytes=64)
-            scales = ring5.tile([P, 2 * C], U8, name="da_s", align_bytes=64)
+            codes = ring5.tile([P, 2 * C], U32, name="da_c", align_bytes=64, bufs=PR["da_c"])
+            scales = ring5.tile([P, 2 * C], U8, name="da_s", align_bytes=64, bufs=PR["da_c"])
             nc.vector.quantize_mx(
                 out=codes[:].bitcast(FP8X4), scales=scales[:], in_=da_b[u][:].rearrange("p a c -> p (a c)")
             )
-            da_codes[divmod(u, HALVES)] = codes
-            da_scales[divmod(u, HALVES)] = scales
+            da_codes[order[u]] = codes
+            da_scales[order[u]] = scales
 
         def load13(e, m, k0, k1, halves=(0, 1)):
-            if k1 - k0 > 0:
-                for h in halves:
-                    raw = wraw.tile([P, PACK, k1 - k0], F32, name="w_raw", bufs=PR["wraw"])
-                    rows = (w1, w3)[m][e][h * PASS : (h + 1) * PASS, k0:k1]
-                    nc.sync.dma_start(raw[:], rows.rearrange("(p j) k -> p j k", j=PACK))
-                    raw13[(e, m, h, k0)] = raw[:]
-            else:
-                raw = wraw.tile([P, HALVES, PACK, k1 - k0], F32, name="w_raw", bufs=PR["wraw"])
-                for h in range(HALVES):
-                    rows = (w1, w3)[m][e][h * PASS : (h + 1) * PASS, k0:k1]
-                    nc.sync.dma_start(raw[:, h], rows.rearrange("(p j) k -> p j k", j=PACK))
-                    raw13[(e, m, h, k0)] = raw[:, h]
+            for h in halves:
+                raw = wraw.tile([P, PACK, k1 - k0], F32, name="w_raw", bufs=PR["wraw"])
+                rows = (w1, w3)[m][e][h * PASS : (h + 1) * PASS, k0:k1]
+                nc.sync.dma_start(raw[:], rows.rearrange("(p j) k -> p j k", j=PACK))
+                for kt in range(k0 // P, k1 // P):
+                    raw13[(e, m, h, kt * P)] = raw[:, :, kt * P - k0 :]
 
         w13_c = {}
         w13_s = {}
@@ -204,9 +215,9 @@ def tile_moe_bdx_glu_silu_kernel(
             words = HALVES * width
             w_b = ring3.tile([P, words * PACK], BF16, name="w13_b", align_bytes=64, bufs=PR["w13_b"])
             for h in range(HALVES):
-                cast(on_vector, w_b[:, h * width * PACK : (h + 1) * width * PACK], raw13[(e, m, h, k0)], m == 0)
-            w_c = ring4.tile([P, words], U32, name="w13_c", align_bytes=64)
-            w_s = ring4.tile([P, words], U8, name="w13_s", align_bytes=64)
+                cast(on_vector, w_b[:, h * width * PACK : (h + 1) * width * PACK], raw13[(e, m, h, k0)][:, :, :width], m == 0)
+            w_c = ring4.tile([P, words], U32, name="w13_c", align_bytes=64, bufs=PR["w13_c"])
+            w_s = ring4.tile([P, words], U8, name="w13_s", align_bytes=64, bufs=PR["w13_c"])
             for c0 in range(0, words, QUANT // PACK):
                 c1 = min(words, c0 + QUANT // PACK)
                 nc.vector.quantize_mx(
@@ -233,73 +244,104 @@ def tile_moe_bdx_glu_silu_kernel(
                     )
                 nc.scalar.copy(dx[kt][:, e * C : (e + 1) * C], acc[:])
 
-        def combine(kt):
-            first = ring2.tile([P, T], F32, name="first")
-            second = ring2.tile([P, T], F32, name="second")
-            nc.vector.tensor_copy(first[:], dx[kt][:].indirect(pos1_sb[:]))
-            nc.vector.tensor_copy(second[:], dx[kt][:].indirect(pos2_sb[:]))
-            nc.vector.tensor_tensor(first[:], first[:], second[:], ALU.add)
-            nc.sync.dma_start(out[kt * P : (kt + 1) * P, :], first[:])
+        def combine(kt, t0, t1):
+            first = ring3.tile([P, t1 - t0], F32, name="th", bufs=PR["th"])
+            second = ring3.tile([P, t1 - t0], F32, name="z", bufs=PR["z"])
+            nc.vector.tensor_copy(first[:], dx[kt][:].indirect(pos1_sb[:, t0 // 16 : t1 // 16]))
+            nc.vector.tensor_copy(second[:], dx[kt][:].indirect(pos2_sb[:, t0 // 16 : t1 // 16]))
+            adder = nc.gpsimd if kt < PR["gadd"] else nc.vector
+            adder.tensor_tensor(first[:], first[:], second[:], ALU.add)
+            nc.sync.dma_start(out[kt * P : (kt + 1) * P, t0:t1], first[:])
 
         units = E * HALVES
-        last = E - 1
-        VCAST, early, late, B, A = PR["vc"], PR["early"], PR["late"], PR["B"], PR["A"]
-        load_saved(0, 0)
-        load_w2(0)
-        load_gate()
-        load_saved(0, 1)
+        share, early, loaded, late = PR["vc"], PR["early"], PR["loaded"], PR["late"]
+        A, M, B, D = PR["A"], PR["M"], PR["B"], PR["D"]
+
+        def load_w2_for(j):
+            e, h = divmod(j, HALVES)
+            if j < units and e < PR["w2split"]:
+                load_w2(e, (h,))
+            elif j < units and h == 0:
+                load_w2(e, (0, 1))
+
+        for step in PR["head"]:
+            if step == "a1":
+                load_saved(0, 0)
+            if step == "w2":
+                load_w2_for(0)
+            if step == "gate":
+                load_gate()
+            if step == "a3":
+                load_saved(0, 1)
+            if step == "dy":
+                load_dy()
         gather_gradients(0)
         activations(0)
-        quantise_w2(0, VCAST[0])
+        times_up(0)
+        quantise_w2(0, share[0])
         first_product(0)
-        for u in range(1, A):
-            load_w2(u)
-            gather_gradients(u // 2) if u % 2 == 0 else None
-            quantise_w2(u, VCAST[u])
+        for j in range(1, A + PR["LW"]):
+            load_w2_for(j)
+        for j in range(1, A):
+            quantise_w2(j, share[j])
+        for e in range(1, E):
+            gather_gradients(e)
+        for u in range(1, M):
             first_product(u)
-        for b in range(0, -B):
-            load13(*divmod(b, HALVES), 0, early[b // HALVES])
-            quantise13(*divmod(b, HALVES), 0, early[b // HALVES])
-        for u in range(units + max(B, 0)):
+        da_done, w_done, backs = {}, {}, []
+        for u in range(units + max(B, 0) + D):
             b = u - B
-            d = u - max(B, 0) - PR["D"]
             for step in PR["loads"]:
-                if step == "w2" and u + A < units:
-                    load_w2(u + A)
-                if step == "a1" and u + 1 < units:
-                    load_saved(u + 1, 0)
-                if step == "a3" and u + 1 < units:
-                    load_saved(u + 1, 1)
+                if step == "w2":
+                    load_w2_for(u + A + PR["LW"])
+                for which in range(2):
+                    ahead = u + 1 + PR["LA"]
+                    if step == ("a1", "a3")[which]:
+                        for x in range(1, min(ahead, units - 1) + 1):
+                            if x not in (v, up)[which]:
+                                load_saved(x, which)
                 if step in ("h0", "h1") and 0 <= b < units:
-                    load13(*divmod(b, HALVES), 0, early[b // HALVES], (int(step[1]),))
+                    load13(*divmod(b, HALVES), 0, loaded[b // HALVES], (int(step[1]),))
             if u == 2:
                 nc.sync.dma_start(pos1_sb[:], pos1)
                 nc.sync.dma_start(pos2_sb[:], pos2)
-            if (u + A) % 2 == 0 and u + A < units:
-                gather_gradients((u + A) // 2)
             for step in PR["steps"]:
                 if step == "q" and u < units:
                     times_sigmoid(u)
                 if step == "qw2" and u + A < units:
-                    quantise_w2(u + A, VCAST[u + A])
+                    quantise_w2(u + A, share[u + A])
                 if step == "da" and u < units:
                     products(u)
                 if step == "act" and u + 1 < units:
                     activations(u + 1)
-                if step == "mm1" and u + A < units:
-                    first_product(u + A)
+                if step == "z" and u + 1 < units:
+                    times_up(u + 1)
+                if step == "mm1" and u + M < units:
+                    first_product(u + M)
                 if step == "q13" and 0 <= b < units:
-                    quantise13(*divmod(b, HALVES), 0, early[b // HALVES])
+                    quantise13(*divmod(b, HALVES), 0, early[b // HALVES], (b, 0) in PR["lv"])
+                    w_done[divmod(b, HALVES)] = u
                 if step == "qda" and u < units:
                     quantise_da(u)
-                if step == "back" and d >= 0 and d % HALVES == 1:
-                    back(d // HALVES, 0, early[d // HALVES])
-        if PR["D"] == 1:
-            back(last, 0, early[last])
+                    da_done[order[u]] = u
+                if step == "back":
+                    for e in range(E):
+                        stamps = [done.get((e, x), u + 1) for done in (da_done, w_done) for x in range(2)]
+                        if e not in backs and max(stamps) + D <= u:
+                            back(e, 0, early[e])
+                            backs.append(e)
+        for e in range(E):
+            if e not in backs:
+                back(e, 0, early[e])
         for e, kt in late:
             for m in range(2):
-                load13(e, m, kt * P, (kt + 1) * P)
-                quantise13(e, m, kt * P, (kt + 1) * P, (e, kt, m) in PR["lv"])
+                if kt * P >= loaded[e]:
+                    load13(e, m, kt * P, (kt + 1) * P)
+                quantise13(e, m, kt * P, (kt + 1) * P, (HALVES * e + m, kt) in PR["lv"])
             back(e, kt * P, (kt + 1) * P)
         for kt in range(K_TILES):
-            combine(kt)
+            if kt == K_TILES - 1 and PR["cut"]:
+                combine(kt, 0, PR["cut"])
+                combine(kt, PR["cut"], T)
+            else:
+                combine(kt, 0, T)

@@ -3,7 +3,7 @@ from contextlib import ExitStack
 import concourse.mybir as mybir
 from concourse.masks import make_identity
 
-PR = {'sums': 2, 'turned': 2, 'acc': 4, 'gated': 4, 'q': 3, 'z': 2, 'th': 3, 'v': 3, 'up': 1, 'w2_b': 2, 'w2_c': 3, 'da_b': 1, 'w13_b': 3, 'wraw': 8, 'w2raw': 2, 'da_c': 6, 'w13_c': 5, 'vc': (0, 384, 0, 512, 512, 0, 512, 512, 512, 512), 'early': (384, 384, 384, 384, 128), 'loaded': (384, 384, 384, 384, 128), 'late': ((4, 1), (4, 2)), 'B': 1, 'A': 4, 'M': 1, 'D': 3, 'LW': 3, 'LA': 0, 'lv': ((5, 1), (6, 0), (6, 1), (8, 2), (9, 1)), 'w2split': 0, 'chunks': ((0,), (1, 2), (3, 4)), 'loads': ['a1', 'w2', 'a3', 'h0', 'h1'], 'steps': ['q', 'da', 'qda', 'q13', 'mm1', 'qw2', 'act', 'back', 'z'], 'gadd': 0, 'cut': 448, 'head': ['dy', 'w2', 'a1', 'gate', 'a3'], 'fix': 1}
+PR = {'sums': 2, 'turned': 3, 'acc': 3, 'gated': 8, 'q': 11, 'z': 2, 'th': 3, 'v': 4, 'up': 2, 'w2_b': 5, 'w2_c': 2, 'da_b': 1, 'w13_b': 4, 'wraw': 7, 'w2raw': 2, 'da_c': 4, 'w13_c': 3, 'vc': (0, 512, 128, 512, 128, 512, 128, 512, 128, 256), 'early': (384, 384, 384, 256, 256), 'loaded': (384, 384, 384, 256, 256), 'late': ((3, 2), (4, 2)), 'B': 1, 'A': 3, 'M': 1, 'D': 3, 'LW': 0, 'LA': 0, 'lv': ((6, 1), (7, 2), (8, 1), (9, 1)), 'w2split': 2, 'chunks': ((0,), (1,), (2,), (3,), (4,)), 'loads': ['a1', 'h0', 'h1', 'w2', 'a3'], 'steps': ['q13', 'qw2', 'q', 'da', 'act', 'qda', 'back', 'mm1', 'z'], 'gadd': 0, 'cut': 320, 'head': ['dy', 'w2', 'a1', 'a3', 'gate'], 'fix': 0}
 K, T, E, C, H, N = 384, 640, 5, 256, 1024, 512
 S = E * C
 
@@ -29,11 +29,11 @@ QUANT = 2048
 
 
 def by_fours_out(ap):
-    return ap.rearrange("p (c i t) -> p c t i", i=2, t=PACK)
+    return ap.rearrange("p (c i t) -> p c t i", i=4, t=PACK)
 
 
 def by_fours_in(ap):
-    return ap.rearrange("p t (c i) -> p c t i", i=2)
+    return ap.rearrange("p t (c i) -> p c t i", i=4)
 
 
 def tile_moe_bdx_glu_silu_kernel(

@@ -3,7 +3,7 @@ from contextlib import ExitStack
 import concourse.mybir as mybir
 from concourse.masks import make_identity
 
-PR = {'sums': 2, 'turned': 3, 'acc': 3, 'gated': 8, 'q': 11, 'z': 2, 'th': 3, 'v': 4, 'up': 2, 'w2_b': 5, 'w2_c': 2, 'da_b': 1, 'w13_b': 4, 'wraw': 7, 'w2raw': 2, 'da_c': 4, 'w13_c': 3, 'vc': (0, 512, 128, 512, 128, 512, 128, 512, 128, 256), 'early': (384, 384, 384, 256, 256), 'loaded': (384, 384, 384, 256, 256), 'late': ((3, 2), (4, 2)), 'B': 1, 'A': 3, 'M': 1, 'D': 3, 'LW': 0, 'LA': 0, 'lv': ((6, 1), (7, 2), (8, 1), (9, 1)), 'w2split': 2, 'chunks': ((0,), (1,), (2,), (3,), (4,)), 'loads': ['a1', 'h0', 'h1', 'w2', 'a3'], 'steps': ['q13', 'qw2', 'q', 'da', 'act', 'qda', 'back', 'mm1', 'z'], 'gadd': 0, 'cut': 320, 'head': ['dy', 'w2', 'a1', 'a3', 'gate'], 'fix': 0}
+PR = {'sums': 3, 'turned': 2, 'acc': 3, 'gated': 3, 'q': 17, 'z': 3, 'th': 4, 'v': 3, 'up': 1, 'w2_b': 1, 'w2_c': 1, 'da_b': 5, 'w13_b': 3, 'wraw': 7, 'w2raw': 2, 'da_c': 5, 'w13_c': 5, 'vc': (0, 384, 128, 384, 0, 512, 128, 512, 128, 512), 'early': (384, 384, 384, 384, 128), 'loaded': (384, 384, 384, 384, 128), 'late': ((4, 1), (4, 2)), 'B': 1, 'A': 3, 'M': 2, 'D': 4, 'LW': 0, 'LA': 0, 'lv': ((5, 1), (5, 2), (6, 2), (7, 1), (7, 2), (9, 1)), 'w2split': 1, 'chunks': ((0,), (1,), (2,), (3,), (4,)), 'loads': ['a1', 'h0', 'h1', 'w2', 'a3'], 'steps': ['qw2', 'q13', 'act', 'z', 'q', 'da', 'qda', 'back', 'mm1'], 'gadd': 2, 'cut': 448, 'head': ['dy', 'a3', 'gate', 'w2', 'a1'], 'fix': 0, 'mw2': (1, 3, 4), 'm13': 0, 'ZL': 0}
 K, T, E, C, H, N = 384, 640, 5, 256, 1024, 512
 S = E * C
 
@@ -125,15 +125,26 @@ def tile_moe_bdx_glu_silu_kernel(
             for n, member in enumerate(group):
                 (v, up)[which][order.index((member, h))] = dst[:, :, n * C : (n + 1) * C]
 
+        w2_b = {}
+
         def quantise_w2(u, split):
-            w2_b = ring2.tile([P, PASS * PACK], BF16, name="w2_b", align_bytes=64, bufs=PR["w2_b"])
+            e, h = divmod(u, HALVES)
+            halves = (0, 1) if e in PR["mw2"] else (h,)
+            n = halves.index(h)
+            if n == 0:
+                w2_b[u] = ring2.tile([P, len(halves) * PASS * PACK], BF16, name="w2_b", align_bytes=64, bufs=PR["w2_b"])
+            dst = w2_b[u - n][:, n * PASS * PACK : (n + 1) * PASS * PACK]
             if split < PASS:
-                cast(False, w2_b[:, split * PACK :], w2_raw[u][:, :, split:], False)
+                cast(False, dst[:, split * PACK :], w2_raw[u][:, :, split:], False)
             if split > 0:
-                cast(True, w2_b[:, : split * PACK], w2_raw[u][:, :, :split], False)
-            w2_c[u] = ring2.tile([P, PASS], U32, name="w2_c", align_bytes=64, bufs=PR["w2_c"])
-            w2_s[u] = ring2.tile([P, PASS], U8, name="w2_s", align_bytes=64, bufs=PR["w2_c"])
-            nc.vector.quantize_mx(out=w2_c[u][:].bitcast(FP8X4), scales=w2_s[u][:], in_=w2_b[:])
+                cast(True, dst[:, : split * PACK], w2_raw[u][:, :, :split], False)
+            if h == halves[-1]:
+                codes = ring2.tile([P, len(halves) * PASS], U32, name="w2_c", align_bytes=64, bufs=PR["w2_c"])
+                scales = ring2.tile([P, len(halves) * PASS], U8, name="w2_s", align_bytes=64, bufs=PR["w2_c"])
+                nc.vector.quantize_mx(out=codes[:].bitcast(FP8X4), scales=scales[:], in_=w2_b[u - n][:])
+                for x in range(len(halves)):
+                    w2_c[u - n + x] = codes[:, x * PASS : (x + 1) * PASS]
+                    w2_s[u - n + x] = scales[:, x * PASS : (x + 1) * PASS]
 
         def activations(u):
             z[u] = ring3.tile([P, PACK, C], F32, name="z", bufs=PR["z"])
@@ -156,8 +167,8 @@ def tile_moe_bdx_glu_silu_kernel(
                     out=sums[:],
                     lhsT=g_w[e][:, cols].bitcast(FP8X4),
                     lhsT_scale=g_s[e][:, cols],
-                    rhs=w2_c[j][:].bitcast(FP8X4),
-                    rhs_scale=w2_s[j][:],
+                    rhs=w2_c[j].bitcast(FP8X4),
+                    rhs_scale=w2_s[j],
                     start=True,
                     stop=True,
                 )
@@ -210,21 +221,34 @@ def tile_moe_bdx_glu_silu_kernel(
         w13_c = {}
         w13_s = {}
 
+        w13_b = {}
+
         def quantise13(e, m, k0, k1, on_vector=False):
             width = k1 - k0
             words = HALVES * width
-            w_b = ring3.tile([P, words * PACK], BF16, name="w13_b", align_bytes=64, bufs=PR["w13_b"])
-            for h in range(HALVES):
-                cast(on_vector, w_b[:, h * width * PACK : (h + 1) * width * PACK], raw13[(e, m, h, k0)][:, :, :width], m == 0)
-            w_c = ring4.tile([P, words], U32, name="w13_c", align_bytes=64, bufs=PR["w13_c"])
-            w_s = ring4.tile([P, words], U8, name="w13_s", align_bytes=64, bufs=PR["w13_c"])
-            for c0 in range(0, words, QUANT // PACK):
-                c1 = min(words, c0 + QUANT // PACK)
-                nc.vector.quantize_mx(
-                    out=w_c[:, c0:c1].bitcast(FP8X4), scales=w_s[:, c0:c1], in_=w_b[:, PACK * c0 : PACK * c1]
+            both = (0, 1) if PR["m13"] else (m,)
+            n = both.index(m)
+            if n == 0:
+                w13_b[(e, k0)] = ring3.tile(
+                    [P, len(both) * words * PACK], BF16, name="w13_b", align_bytes=64, bufs=PR["w13_b"]
                 )
-            w13_c[(e, m, k0)] = w_c
-            w13_s[(e, m, k0)] = w_s
+            w_b = w13_b[(e, k0)]
+            for h in range(HALVES):
+                c0 = (n * words + h * width) * PACK
+                cast(on_vector, w_b[:, c0 : c0 + width * PACK], raw13[(e, m, h, k0)][:, :, :width], m == 0)
+            if m == both[-1]:
+                total = len(both) * words
+                w_c = ring4.tile([P, total], U32, name="w13_c", align_bytes=64, bufs=PR["w13_c"])
+                w_s = ring4.tile([P, total], U8, name="w13_s", align_bytes=64, bufs=PR["w13_c"])
+                widest = 1024 if total >= 1024 else 512
+                for c0 in range(0, total, widest):
+                    c1 = min(total, c0 + widest)
+                    nc.vector.quantize_mx(
+                        out=w_c[:, c0:c1].bitcast(FP8X4), scales=w_s[:, c0:c1], in_=w_b[:, PACK * c0 : PACK * c1]
+                    )
+                for x, member in enumerate(both):
+                    w13_c[(e, member, k0)] = w_c[:, x * words : (x + 1) * words]
+                    w13_s[(e, member, k0)] = w_s[:, x * words : (x + 1) * words]
 
         def back(e, k0, k1):
             width = k1 - k0
@@ -314,13 +338,14 @@ def tile_moe_bdx_glu_silu_kernel(
                     products(u)
                 if step == "act" and u + 1 < units:
                     activations(u + 1)
-                if step == "z" and u + 1 < units:
-                    times_up(u + 1)
+                if step == "z" and 0 < u + PR["ZL"] < units:
+                    times_up(u + PR["ZL"])
                 if step == "mm1" and u + M < units:
                     first_product(u + M)
                 if step == "q13" and 0 <= b < units:
                     quantise13(*divmod(b, HALVES), 0, early[b // HALVES], (b, 0) in PR["lv"])
-                    w_done[divmod(b, HALVES)] = u
+                    for key in w13_c:
+                        w_done.setdefault(key[:2], u)
                 if step == "qda" and u < units:
                     quantise_da(u)
                     da_done[order[u]] = u

from contextlib import ExitStack

import concourse.mybir as mybir
from concourse.masks import make_identity

PR = {'sums': 3, 'turned': 2, 'acc': 3, 'gated': 3, 'q': 17, 'z': 3, 'th': 4, 'v': 3, 'up': 1, 'w2_b': 1, 'w2_c': 1, 'da_b': 5, 'w13_b': 3, 'wraw': 7, 'w2raw': 2, 'da_c': 5, 'w13_c': 5, 'vc': (0, 384, 128, 384, 0, 512, 128, 512, 128, 512), 'early': (384, 384, 384, 384, 128), 'loaded': (384, 384, 384, 384, 128), 'late': ((4, 1), (4, 2)), 'B': 1, 'A': 3, 'M': 2, 'D': 4, 'LW': 0, 'LA': 0, 'lv': ((5, 1), (5, 2), (6, 2), (7, 1), (7, 2), (9, 1)), 'w2split': 1, 'chunks': ((0,), (1,), (2,), (3,), (4,)), 'loads': ['a1', 'h0', 'h1', 'w2', 'a3'], 'steps': ['qw2', 'q13', 'act', 'z', 'q', 'da', 'qda', 'back', 'mm1'], 'gadd': 2, 'cut': 448, 'head': ['dy', 'a3', 'gate', 'w2', 'a1'], 'fix': 0, 'mw2': (1, 3, 4), 'm13': 0, 'ZL': 0}
K, T, E, C, H, N = 384, 640, 5, 256, 1024, 512
S = E * C

FLOPS = 2 * S * (N * H + 2 * H * K)
BYTES = 4 * (2 * H * S + E * N * H + 2 * E * H * K + S + K * T) + N * T + 16 * T + 2 * 128 * (S + 2 * T) // 16

F32 = mybir.dt.float32
BF16 = mybir.dt.bfloat16
I32 = mybir.dt.int32
U32 = mybir.dt.uint32
U16 = mybir.dt.uint16
U8 = mybir.dt.uint8
FP8X4 = mybir.dt.float8_e4m3fn_x4
ALU = mybir.AluOpType
ACT = mybir.ActivationFunctionType

P = 128
PACK = 4
PASS = P * PACK
HALVES = H // PASS
K_TILES = K // P
QUANT = 2048


def by_fours_out(ap):
    return ap.rearrange("p (c i t) -> p c t i", i=4, t=PACK)


def by_fours_in(ap):
    return ap.rearrange("p t (c i) -> p c t i", i=4)


def tile_moe_bdx_glu_silu_kernel(
    tc, dy_words, dy_scales, a1, a3, w2, w1, w3, gate, offs, pos1, pos2, out
):
    nc = tc.nc
    with ExitStack() as ctx:
        held = ctx.enter_context(tc.tile_pool(name="held", bufs=1))
        ring2 = ctx.enter_context(tc.tile_pool(name="ring2", bufs=2))
        ring3 = ctx.enter_context(tc.tile_pool(name="ring3", bufs=3))
        ring4 = ctx.enter_context(tc.tile_pool(name="ring4", bufs=4))
        ring5 = ctx.enter_context(tc.tile_pool(name="ring5", bufs=5))
        wraw = ctx.enter_context(tc.tile_pool(name="wraw", bufs=8))
        w2pool = ctx.enter_context(tc.tile_pool(name="w2pool", bufs=2))
        psum4 = ctx.enter_context(tc.psum_pool(name="psum4", bufs=4))
        psum2 = ctx.enter_context(tc.psum_pool(name="psum2", bufs=2))

        offs_sb = held.tile([P, S // 16], U16, name="offs_sb")
        pos1_sb = held.tile([P, T // 16], U16, name="pos1_sb")
        pos2_sb = held.tile([P, T // 16], U16, name="pos2_sb")
        dy_w = held.tile([P, T], I32, name="dy_w", align_bytes=64)
        dy_s = held.tile([P, T], U8, name="dy_s", align_bytes=64)
        gate_rows = held.tile([P, P], F32, name="gate_rows")
        ident = held.tile([P, P], F32, name="ident")
        half_gate = held.tile([P, S // P], F32, name="half_gate")
        g_w = [held.tile([P, C], U32, name="g_w%d" % e, align_bytes=64) for e in range(E)]
        g_s = [held.tile([P, C], U8, name="g_s%d" % e, align_bytes=64) for e in range(E)]
        dx = [held.tile([P, S], F32, name="dx%d" % kt, align_bytes=64) for kt in range(K_TILES)]

        make_identity(nc, ident[:])


        def load_dy():
            nc.sync.dma_start(offs_sb[:], offs)
            nc.sync.dma_start(dy_w[:], dy_words[0].rearrange("p t d -> p (t d)").bitcast(I32))
            for quad in range(4):
                rows = dy_scales[0, 4 * quad : 4 * quad + 4, :].bitcast(I32)
                nc.sync.dma_start(
                    dy_s[32 * quad : 32 * quad + 32, :].bitcast(I32), rows.unsqueeze(0).broadcast_to([8, 4, T // 4])
                )

        def load_gate():
            nc.sync.dma_start(gate_rows[:], gate.rearrange("i (c p) -> (i c) p", p=P)[0:P, :])
            gate_ps = psum4.tile([P, PACK, P], F32, name="turned", bufs=PR["turned"])
            nc.tensor.transpose(gate_ps[:, 0, :], gate_rows[:], ident[:])
            nc.scalar.activation(half_gate[:], gate_ps[:, 0, 0 : S // P], ACT.Copy, scale=0.5)

        da_codes = {}
        da_scales = {}
        raw13 = {}

        def gather_gradients(e):
            entries = offs_sb[:, e * (C // 16) : (e + 1) * (C // 16)]
            nc.vector.tensor_copy(g_w[e][:], dy_w[:].bitcast(U32).indirect(entries))
            nc.vector.tensor_copy(g_s[e][:], dy_s[:].indirect(entries))

        def cast(on_vector, dst, src, negate):
            if on_vector and negate:
                nc.vector.tensor_scalar(by_fours_out(dst), by_fours_in(src), -1.0, None, ALU.mult)
            elif on_vector:
                nc.vector.tensor_copy(by_fours_out(dst), by_fours_in(src))
            else:
                nc.scalar.activation(by_fours_out(dst), by_fours_in(src), ACT.Copy, scale=-1.0 if negate else 1.0)

        order = [(e, h) for group in PR["chunks"] for h in range(HALVES) for e in group]
        w2_raw, v, up, th, z, q, w2_c, w2_s = {}, {}, {}, {}, {}, {}, {}, {}

        def load_w2(e, halves):
            if len(halves) == HALVES:
                raw = w2pool.tile([P, PACK, H], F32, name="w2_raw", bufs=PR["w2raw"])
                nc.sync.dma_start(raw[:], w2[e].rearrange("(p j) c -> p j c", j=PACK))
                for h in halves:
                    w2_raw[HALVES * e + h] = raw[:, :, h * PASS : (h + 1) * PASS]
            else:
                h = halves[0]
                raw = w2pool.tile([P, PACK, PASS], F32, name="w2_raw", bufs=PR["w2raw"])
                nc.sync.dma_start(raw[:], w2[e][:, h * PASS : (h + 1) * PASS].rearrange("(p j) c -> p j c", j=PACK))
                w2_raw[HALVES * e + h] = raw[:]

        def load_saved(u, which):
            e, h = order[u]
            group = [g for g in PR["chunks"] if e in g][0]
            src = (a1, a3)[which][h * PASS : (h + 1) * PASS, group[0] * C : (group[-1] + 1) * C]
            if which == 0:
                dst = ring4.tile([P, PACK, len(group) * C], F32, name="v", bufs=PR["v"])
            else:
                dst = ring3.tile([P, PACK, len(group) * C], F32, name="up", bufs=PR["up"])
            nc.sync.dma_start(dst[:], src.rearrange("(p t) c -> p t c", t=PACK))
            for n, member in enumerate(group):
                (v, up)[which][order.index((member, h))] = dst[:, :, n * C : (n + 1) * C]

        w2_b = {}

        def quantise_w2(u, split):
            e, h = divmod(u, HALVES)
            halves = (0, 1) if e in PR["mw2"] else (h,)
            n = halves.index(h)
            if n == 0:
                w2_b[u] = ring2.tile([P, len(halves) * PASS * PACK], BF16, name="w2_b", align_bytes=64, bufs=PR["w2_b"])
            dst = w2_b[u - n][:, n * PASS * PACK : (n + 1) * PASS * PACK]
            if split < PASS:
                cast(False, dst[:, split * PACK :], w2_raw[u][:, :, split:], False)
            if split > 0:
                cast(True, dst[:, : split * PACK], w2_raw[u][:, :, :split], False)
            if h == halves[-1]:
                codes = ring2.tile([P, len(halves) * PASS], U32, name="w2_c", align_bytes=64, bufs=PR["w2_c"])
                scales = ring2.tile([P, len(halves) * PASS], U8, name="w2_s", align_bytes=64, bufs=PR["w2_c"])
                nc.vector.quantize_mx(out=codes[:].bitcast(FP8X4), scales=scales[:], in_=w2_b[u - n][:])
                for x in range(len(halves)):
                    w2_c[u - n + x] = codes[:, x * PASS : (x + 1) * PASS]
                    w2_s[u - n + x] = scales[:, x * PASS : (x + 1) * PASS]

        def activations(u):
            z[u] = ring3.tile([P, PACK, C], F32, name="z", bufs=PR["z"])
            nc.scalar.activation(z[u][:], v[u], ACT.Silu, scale=-1.0)
            th[u] = ring3.tile([P, PACK, C], F32, name="th", bufs=PR["th"])
            nc.scalar.activation(th[u][:], v[u], ACT.Tanh, scale=0.5)

        def times_up(u):
            nc.vector.scalar_tensor_tensor(z[u][:], z[u][:], 1.0, up[u], ALU.subtract, ALU.mult)

        turned = {}

        def first_product(u):
            e, h = order[u]
            j = HALVES * e + h
            for s in range(C // P):
                cols = slice(s * P, (s + 1) * P)
                sums = psum2.tile([P, PASS], F32, name="sums", bufs=PR["sums"])
                nc.tensor.matmul_mx(
                    out=sums[:],
                    lhsT=g_w[e][:, cols].bitcast(FP8X4),
                    lhsT_scale=g_s[e][:, cols],
                    rhs=w2_c[j].bitcast(FP8X4),
                    rhs_scale=w2_s[j],
                    start=True,
                    stop=True,
                )
                gated = ring4.tile([P, PACK, P], F32, name="gated", bufs=PR["gated"])
                block = e * (C // P) + s
                nc.scalar.activation(
                    gated[:],
                    sums[:].rearrange("p (m t) -> p t m", t=PACK),
                    ACT.Copy,
                    scale=half_gate[:, block : block + 1],
                )
                turned[(u, s)] = psum4.tile([P, PACK, P], F32, name="turned", bufs=PR["turned"])
                for t in range(PACK):
                    nc.tensor.transpose(turned[(u, s)][:, t, :], gated[:, t, :], ident[:])

        def times_sigmoid(u):
            q[u] = th[u]
            for s in range(C // P):
                cols = slice(s * P, (s + 1) * P)
                nc.vector.scalar_tensor_tensor(
                    q[u][:, :, cols], th[u][:, :, cols], 1.0, turned[(u, s)][:], ALU.add, ALU.mult
                )

        da_b = {}

        def products(u):
            da_b[u] = ring2.tile([P, 2, C * PACK], BF16, name="da_b", align_bytes=64, bufs=PR["da_b"])
            for m, factor in enumerate((z[u][:], v[u])):
                nc.vector.tensor_tensor(
                    by_fours_out(da_b[u][:, m, :]), by_fours_in(q[u][:]), by_fours_in(factor), ALU.mult
                )

        def quantise_da(u):
            codes = ring5.tile([P, 2 * C], U32, name="da_c", align_bytes=64, bufs=PR["da_c"])
            scales = ring5.tile([P, 2 * C], U8, name="da_s", align_bytes=64, bufs=PR["da_c"])
            nc.vector.quantize_mx(
                out=codes[:].bitcast(FP8X4), scales=scales[:], in_=da_b[u][:].rearrange("p a c -> p (a c)")
            )
            da_codes[order[u]] = codes
            da_scales[order[u]] = scales

        def load13(e, m, k0, k1, halves=(0, 1)):
            for h in halves:
                raw = wraw.tile([P, PACK, k1 - k0], F32, name="w_raw", bufs=PR["wraw"])
                rows = (w1, w3)[m][e][h * PASS : (h + 1) * PASS, k0:k1]
                nc.sync.dma_start(raw[:], rows.rearrange("(p j) k -> p j k", j=PACK))
                for kt in range(k0 // P, k1 // P):
                    raw13[(e, m, h, kt * P)] = raw[:, :, kt * P - k0 :]

        w13_c = {}
        w13_s = {}

        w13_b = {}

        def quantise13(e, m, k0, k1, on_vector=False):
            width = k1 - k0
            words = HALVES * width
            both = (0, 1) if PR["m13"] else (m,)
            n = both.index(m)
            if n == 0:
                w13_b[(e, k0)] = ring3.tile(
                    [P, len(both) * words * PACK], BF16, name="w13_b", align_bytes=64, bufs=PR["w13_b"]
                )
            w_b = w13_b[(e, k0)]
            for h in range(HALVES):
                c0 = (n * words + h * width) * PACK
                cast(on_vector, w_b[:, c0 : c0 + width * PACK], raw13[(e, m, h, k0)][:, :, :width], m == 0)
            if m == both[-1]:
                total = len(both) * words
                w_c = ring4.tile([P, total], U32, name="w13_c", align_bytes=64, bufs=PR["w13_c"])
                w_s = ring4.tile([P, total], U8, name="w13_s", align_bytes=64, bufs=PR["w13_c"])
                widest = 1024 if total >= 1024 else 512
                for c0 in range(0, total, widest):
                    c1 = min(total, c0 + widest)
                    nc.vector.quantize_mx(
                        out=w_c[:, c0:c1].bitcast(FP8X4), scales=w_s[:, c0:c1], in_=w_b[:, PACK * c0 : PACK * c1]
                    )
                for x, member in enumerate(both):
                    w13_c[(e, member, k0)] = w_c[:, x * words : (x + 1) * words]
                    w13_s[(e, member, k0)] = w_s[:, x * words : (x + 1) * words]

        def back(e, k0, k1):
            width = k1 - k0
            for kt in range(k0 // P, k1 // P):
                acc = psum2.tile([P, C], F32, name="acc", bufs=PR["acc"])
                steps = [(h, m) for m in range(2) for h in range(HALVES)]
                for n, (h, m) in enumerate(steps):
                    c0 = h * width + kt * P - k0
                    nc.tensor.matmul_mx(
                        out=acc[:],
                        lhsT=w13_c[(e, m, k0)][:, c0 : c0 + P].bitcast(FP8X4),
                        lhsT_scale=w13_s[(e, m, k0)][:, c0 : c0 + P],
                        rhs=da_codes[(e, h)][:, m * C : (m + 1) * C].bitcast(FP8X4),
                        rhs_scale=da_scales[(e, h)][:, m * C : (m + 1) * C],
                        start=n == 0,
                        stop=n == len(steps) - 1,
                    )
                nc.scalar.copy(dx[kt][:, e * C : (e + 1) * C], acc[:])

        def combine(kt, t0, t1):
            first = ring3.tile([P, t1 - t0], F32, name="th", bufs=PR["th"])
            second = ring3.tile([P, t1 - t0], F32, name="z", bufs=PR["z"])
            nc.vector.tensor_copy(first[:], dx[kt][:].indirect(pos1_sb[:, t0 // 16 : t1 // 16]))
            nc.vector.tensor_copy(second[:], dx[kt][:].indirect(pos2_sb[:, t0 // 16 : t1 // 16]))
            adder = nc.gpsimd if kt < PR["gadd"] else nc.vector
            adder.tensor_tensor(first[:], first[:], second[:], ALU.add)
            nc.sync.dma_start(out[kt * P : (kt + 1) * P, t0:t1], first[:])

        units = E * HALVES
        share, early, loaded, late = PR["vc"], PR["early"], PR["loaded"], PR["late"]
        A, M, B, D = PR["A"], PR["M"], PR["B"], PR["D"]

        def load_w2_for(j):
            e, h = divmod(j, HALVES)
            if j < units and e < PR["w2split"]:
                load_w2(e, (h,))
            elif j < units and h == 0:
                load_w2(e, (0, 1))

        for step in PR["head"]:
            if step == "a1":
                load_saved(0, 0)
            if step == "w2":
                load_w2_for(0)
            if step == "gate":
                load_gate()
            if step == "a3":
                load_saved(0, 1)
            if step == "dy":
                load_dy()
        gather_gradients(0)
        activations(0)
        times_up(0)
        quantise_w2(0, share[0])
        first_product(0)
        for j in range(1, A + PR["LW"]):
            load_w2_for(j)
        for j in range(1, A):
            quantise_w2(j, share[j])
        for e in range(1, E):
            gather_gradients(e)
        for u in range(1, M):
            first_product(u)
        da_done, w_done, backs = {}, {}, []
        for u in range(units + max(B, 0) + D):
            b = u - B
            for step in PR["loads"]:
                if step == "w2":
                    load_w2_for(u + A + PR["LW"])
                for which in range(2):
                    ahead = u + 1 + PR["LA"]
                    if step == ("a1", "a3")[which]:
                        for x in range(1, min(ahead, units - 1) + 1):
                            if x not in (v, up)[which]:
                                load_saved(x, which)
                if step in ("h0", "h1") and 0 <= b < units:
                    load13(*divmod(b, HALVES), 0, loaded[b // HALVES], (int(step[1]),))
            if u == 2:
                nc.sync.dma_start(pos1_sb[:], pos1)
                nc.sync.dma_start(pos2_sb[:], pos2)
            for step in PR["steps"]:
                if step == "q" and u < units:
                    times_sigmoid(u)
                if step == "qw2" and u + A < units:
                    quantise_w2(u + A, share[u + A])
                if step == "da" and u < units:
                    products(u)
                if step == "act" and u + 1 < units:
                    activations(u + 1)
                if step == "z" and 0 < u + PR["ZL"] < units:
                    times_up(u + PR["ZL"])
                if step == "mm1" and u + M < units:
                    first_product(u + M)
                if step == "q13" and 0 <= b < units:
                    quantise13(*divmod(b, HALVES), 0, early[b // HALVES], (b, 0) in PR["lv"])
                    for key in w13_c:
                        w_done.setdefault(key[:2], u)
                if step == "qda" and u < units:
                    quantise_da(u)
                    da_done[order[u]] = u
                if step == "back":
                    for e in range(E):
                        stamps = [done.get((e, x), u + 1) for done in (da_done, w_done) for x in range(2)]
                        if e not in backs and max(stamps) + D <= u:
                            back(e, 0, early[e])
                            backs.append(e)
        for e in range(E):
            if e not in backs:
                back(e, 0, early[e])
        for e, kt in late:
            for m in range(2):
                if kt * P >= loaded[e]:
                    load13(e, m, kt * P, (kt + 1) * P)
                quantise13(e, m, kt * P, (kt + 1) * P, (HALVES * e + m, kt) in PR["lv"])
            back(e, kt * P, (kt + 1) * P)
        for kt in range(K_TILES):
            if kt == K_TILES - 1 and PR["cut"]:
                combine(kt, 0, PR["cut"])
                combine(kt, PR["cut"], T)
            else:
                combine(kt, 0, T)
